import numpy as np
import ml_dtypes


def mxq(x, axis, fmt="e4m3"):
    dtype, down = {"e4m3": (ml_dtypes.float8_e4m3fn, 7), "e5m2": (ml_dtypes.float8_e5m2, 14)}[fmt]
    v = np.moveaxis(np.asarray(x, np.float32).astype(ml_dtypes.bfloat16).astype(np.float64), axis, -1)
    blocks = v.reshape(v.shape[:-1] + (-1, 32))
    amax = np.abs(blocks).max(-1, keepdims=True)
    byte = np.maximum(np.where(amax > 0, np.frexp(amax)[1] - 1 + 127, 0) - down, 1)
    scale = np.exp2(byte - 127.0)
    codes = (blocks / scale).astype(np.float32).astype(dtype).astype(np.float64)
    return np.moveaxis((codes * scale).reshape(v.shape), -1, axis)


WIDE = False


def mx_kscale(k):
    if not WIDE:
        return np.ones(k)
    levels = np.array([10, -10, 5, -5, 0])
    if k % 512:
        return np.exp2(np.random.permutation(np.resize(levels, k // 32))).repeat(32)
    a = np.empty((k // 512, 16))
    for p in range(k // 512):
        a[p, :8] = np.random.permutation(np.resize(levels, 8))
        for g in range(8):
            far = levels[np.abs(levels - a[p, g]) >= 10]
            a[p, g + 8] = far[np.random.randint(len(far))]
    return np.exp2(a.ravel()).repeat(32)


def f64(x):
    return np.asarray(x).astype(np.float64)


def striped(idx):
    return np.tile(idx.reshape(-1, 16).T, (8, 1)).astype(np.uint16)


def unstriped(offs):
    return offs[:16].T.reshape(-1).astype(np.int64)


def striped8(idx):
    return np.concatenate([x.reshape(-1, 16).T for x in idx]).astype(np.uint16)


def runs(offs, k):
    lists = np.stack([offs[16 * r : 16 * r + 16].T.reshape(-1) for r in range(8)]).astype(np.int64)
    return lists[np.arange(k) % 512 // 64]


def pack_weight(w):
    k, n = w.shape
    w = f64(np.asarray(w, np.float32).astype(ml_dtypes.bfloat16)).reshape(k // 32, 32, n)
    amax = np.abs(w).max(1)
    byte = np.clip(np.where(amax > 0, np.frexp(amax)[1] - 1 + 127 - 7, 1), 1, 254)
    scaled = (w * np.exp2(127.0 - byte)[:, None, :]).reshape(k, n).astype(np.float32)
    words = np.ascontiguousarray(scaled.reshape(k // 512, 128, 4, n).transpose(0, 1, 3, 2)).astype(ml_dtypes.float8_e4m3fn).view(np.uint8)
    return words, np.ascontiguousarray(byte.astype(np.uint8).reshape(k // 512, 16, n))


def unpack_weight(words, scales):
    g, p, n, _ = words.shape
    vals = np.ascontiguousarray(words).view(ml_dtypes.float8_e4m3fn).astype(np.float64) * np.repeat(np.exp2(scales.astype(np.float64) - 127.0), 8, axis=1)[..., None]
    return vals.transpose(0, 1, 3, 2).reshape(g * 512, n)


K, T, S, N, H, G, W = 512, 2048, 512, 512, 512, 2048, 384


def setup_inputs():
    n = np.random.standard_normal
    s = mx_kscale(K)[:, None]
    u = mx_kscale(S)
    packed_xT = pack_weight(n((K, T)) * s)
    packed_dT = pack_weight(n((K, G)) / s)
    return {
        "x_words": packed_xT[0],
        "x_scales": packed_xT[1],
        "w1": (n((K, H)) / np.sqrt(K) / s).astype(np.float32),
        "d_words": packed_dT[0],
        "d_scales": packed_dT[1],
        "gn": (np.random.uniform(0.5, 1.5, (H, 1)) * u[:, None]).astype(np.float32),
        "w2": (n((H, N)) / np.sqrt(H) / u[:, None]).astype(np.float32),
        "offs": striped(np.random.permutation(T)[:S]),
        "k1": striped8(np.random.randint(0, G, (8, H))),
        "two": striped(np.random.permutation(T)[:S]),
        "n1": striped8(np.stack([np.random.permutation(S) for _ in range(8)])),
        "n2": striped8(np.stack([np.random.permutation(S) for _ in range(8)])),
        "n3": striped8(np.stack([np.random.permutation(S) for _ in range(8)])),
        "n4": striped(np.random.permutation(S)[:W]),
        "n5": striped(np.random.permutation(S)[:W]),
    }


def reference(x_words, x_scales, w1, d_words, d_scales, gn, w2, offs, k1, two, n1, n2, n3, n4, n5):
    d_k1 = unpack_weight(d_words, d_scales)[np.arange(K)[:, None], runs(k1, K)]
    x_two = unpack_weight(x_words, x_scales)[:, unstriped(two)]
    d = 0.0625 * (d_k1.T @ x_two)
    xq = unpack_weight(x_words, x_scales)[:, unstriped(offs)]
    y = mxq(f64(w1), 0, "e4m3").T @ xq
    z = f64(gn) * (d * (y[np.arange(H)[:, None], runs(n1, H)] - y) + 0.5 * ((d[np.arange(H)[:, None], runs(n3, H)]) * (y[np.arange(H)[:, None], runs(n2, H)] - y)))
    h = mxq(f64(w2), 0, "e4m3").T @ mxq(z, 0, "e4m3")
    pa = h[:, unstriped(n5)]
    old = h[:, unstriped(n4)]
    ra = np.maximum(pa, 0.5 * old)
    out = h.copy()
    out[:, unstriped(n4)] = ra
    return out

@@ -1,0 +1,216 @@
+from contextlib import ExitStack
+
+import concourse.mybir as mybir
+
+F32 = mybir.dt.float32
+BF16 = mybir.dt.bfloat16
+I32 = mybir.dt.int32
+U32 = mybir.dt.uint32
+U16 = mybir.dt.uint16
+U8 = mybir.dt.uint8
+FP8X4 = mybir.dt.float8_e4m3fn_x4
+ALU = mybir.AluOpType
+COPY = mybir.ActivationFunctionType.Copy
+
+P = 128
+PACK = 4
+T = 2048
+S = 512
+W = 384
+CHUNKS = ((0, 256), (256, 512))
+FLOPS = 3 * 2 * 512 * 512 * 512
+
+
+def tile_picked_twkeyflowbkmax_none_p_kernel(tc, x_words, x_scales, w1, d_words, d_scales, gn, w2, offs, k1, two, n1, n2, n3, n4, n5, out):
+    nc = tc.nc
+    with ExitStack() as ctx:
+        lists = ctx.enter_context(tc.tile_pool(name="lists", bufs=1))
+        sb = ctx.enter_context(tc.tile_pool(name="sb", bufs=1))
+        psum = ctx.enter_context(tc.psum_pool(name="psum", bufs=1))
+
+        def load_list(src, name):
+            t = lists.tile(list(src.shape), U16, name=name)
+            nc.sync.dma_start(t[:], src)
+            return t
+
+        def tile(shape, dtype, name, tag="", bufs=1):
+            return sb.tile(shape, dtype, name=name, tag=tag or name, bufs=bufs, align_bytes=64)
+
+        def load_weight(src, name):
+            t = tile([P, PACK, S], F32, name)
+            nc.sync.dma_start(t[:], src.rearrange("(p j) c -> p j c", j=PACK))
+            return t
+
+        def load_words(src, name):
+            t = tile([P, T], I32, name)
+            nc.sync.dma_start(t[:], src[0].rearrange("p n t -> p (n t)").bitcast(I32))
+            return t
+
+        xs_tab = tile([P, T], U8, "xs_tab")
+        ds_tab = tile([P, T], U8, "ds_tab")
+        nc.vector.memset(ds_tab[:].bitcast(I32), 0)
+        nc.gpsimd.memset(xs_tab[:].bitcast(I32), 0)
+        k1_t = load_list(k1, "k1_t")
+        offs_t = load_list(offs, "offs_t")
+        two_t = load_list(two, "two_t")
+        w1_raw = load_weight(w1, "w1_raw")
+        for e in range(2):
+            nc.scalar.dma_start(ds_tab[e:P:16, :].bitcast(I32), d_scales[0, e:16:2, :].bitcast(I32))
+        for q in range(4):
+            nc.scalar.dma_start(xs_tab[32 * q : 32 * q + 4, :].bitcast(I32), x_scales[0, 4 * q : 4 * q + 4, :].bitcast(I32))
+        xw_tab = load_words(x_words, "xw_tab")
+        n1_t = load_list(n1, "n1_t")
+        n2_t = load_list(n2, "n2_t")
+        dw_tab = load_words(d_words, "dw_tab")
+        w2_raw = load_weight(w2, "w2_raw")
+        n3_t = load_list(n3, "n3_t")
+        n4_t = load_list(n4, "n4_t")
+        n5_t = load_list(n5, "n5_t")
+        gain = tile([P, PACK], F32, "gain")
+        nc.gpsimd.dma_start(gain[:], gn.rearrange("(p j) o -> p (j o)", j=PACK))
+
+        def gather_words(tab, lst, name, tag=""):
+            g = tile([P, S], I32, name, tag)
+            nc.vector.tensor_copy(g[:].bitcast(U32), tab[:].bitcast(U32).indirect(lst[:]))
+            return g
+
+        def gather_bytes(tab, lst, name):
+            g = tile([P, S], U8, name)
+            nc.vector.tensor_copy(g[:], tab[:].indirect(lst[:]))
+            return g
+
+        def quantize(src, n, name):
+            words = tile([P, n], I32, name + "_w")
+            scales = tile([P, n], U8, name + "_s")
+            nc.vector.quantize_mx(words[:].bitcast(FP8X4), scales[:], src)
+            return words, scales
+
+        def product(bank, lw, ls, t, rw, rs):
+            cols = slice(P * t, P * (t + 1))
+            nc.tensor.matmul_mx(bank, lhsT=lw[:, cols].bitcast(FP8X4), lhsT_scale=ls[:, cols], rhs=rw.bitcast(FP8X4), rhs_scale=rs, start=True, stop=True)
+
+        w1_b = tile([P, PACK, P, PACK], BF16, "w1_b")
+        nc.scalar.copy(w1_b[:].rearrange("p t m j -> p m j t"), w1_raw[:].rearrange("p j (m t) -> p m j t", t=PACK))
+        xq_w = gather_words(xw_tab, offs_t, "xq_w")
+        w1_w, w1_s = quantize(w1_b[:].rearrange("p t m j -> p (t m j)"), S, "w1")
+
+        ds_g = gather_bytes(ds_tab, k1_t, "ds_g")
+        xq_s = gather_bytes(xs_tab, offs_t, "xq_s")
+        ds_deal = tile([P, S], U8, "ds_deal")
+        nc.vector.tensor_copy(ds_deal[:].rearrange("p (t m) -> p m t", t=PACK), ds_g[:].rearrange("p (m t) -> p m t", t=PACK))
+        x2_s = gather_bytes(xs_tab, two_t, "x2_s")
+        dk_s = tile([P, S], U8, "dk_s")
+        nc.vector.tensor_copy(dk_s[:].bitcast(I32), ds_deal[:].bitcast(I32))
+        for e in range(2):
+            nc.sync.dma_start(dk_s[2 + e : P : 32, :].bitcast(I32), ds_deal[16 + e : P : 32, :].bitcast(I32))
+
+        y_ps = []
+        for t in range(PACK):
+            bank = psum.tile([P, S], F32, name=f"y_ps{t}", tag=f"bank{t}")
+            product(bank[:], w1_w, w1_s, t, xq_w[:], xq_s[:])
+            y_ps.append(bank)
+
+        x2_w = gather_words(xw_tab, two_t, "x2_w")
+        dw_g = gather_words(dw_tab, k1_t, "dw_g")
+        dk_w = tile([P, S], I32, "dk_w", "work")
+        nc.vector.tensor_copy(dk_w[:].rearrange("p (t m) -> p m t", t=PACK), dw_g[:].rearrange("p (m t) -> p m t", t=PACK))
+
+        gain32 = tile([P, PACK], F32, "gain32")
+        nc.gpsimd.tensor_scalar(gain32[:], gain[:], 0.03125, 0.0, ALU.mult, ALU.add)
+
+        dh = []
+        for t in range(PACK):
+            bank = psum.tile([P, S], F32, name=f"d_ps{t}", tag=f"bank{PACK + t}")
+            product(bank[:], dk_w, dk_s, t, x2_w[:], x2_s[:])
+            d_t = tile([P, S], F32, f"dh{t}")
+            if t < 4:
+                nc.vector.tensor_scalar(d_t[:], bank[:], gain32[:, t : t + 1], None, ALU.mult)
+            else:
+                nc.scalar.activation(d_t[:], bank[:], COPY, scale=gain32[:, t : t + 1])
+            dh.append(d_t)
+
+        w2_b = tile([P, S, PACK], BF16, "w2_b")
+        nc.scalar.copy(w2_b[:].rearrange("p (c i) j -> p c j i", i=4), w2_raw[:].rearrange("p j (c i) -> p c j i", i=4))
+        w2_w, w2_s = quantize(w2_b[:].rearrange("p c j -> p (c j)"), S, "w2")
+
+        y = [tile([P, S], F32, f"y{t}") for t in range(PACK)]
+        h_rows = [tile([P, S], F32, f"h{t}") for t in range(PACK)]
+        own = [tile([P, PACK, c1 - c0], F32, f"own{c0}") for c0, c1 in CHUNKS]
+        far = [tile([P, PACK, c1 - c0], F32, f"far{c0}") for c0, c1 in CHUNKS]
+        diff = tile([P, len(CHUNKS) * PACK, 2, 256], F32, "diff", "work")
+        pairs = {}
+
+        def differences(ci, t):
+            c0, c1 = CHUNKS[ci]
+            n = c1 - c0
+            ent = slice(c0 // 16, c1 // 16)
+            if ci == 0:
+                nc.scalar.copy(y[t][:], y_ps[t][:])
+            pair = tile([P, 2, n], F32, f"pair{ci}_{t}", "pair", 3)
+            nc.scalar.activation(pair[:, 0, :], y[t][:].indirect(n1_t[:, ent]), COPY)
+            nc.scalar.activation(pair[:, 1, :], y[t][:].indirect(n2_t[:, ent]), COPY)
+            pairs[ci, t] = diff[:, PACK * ci + t]
+            nc.vector.tensor_tensor(pairs[ci, t], pair[:], y[t][:, c0:c1].unsqueeze(1).to_broadcast([P, 2, n]), ALU.subtract)
+
+        def products(ci, t):
+            c0, c1 = CHUNKS[ci]
+            ent = slice(c0 // 16, c1 // 16)
+            pair = pairs[ci, t]
+            nc.vector.scalar_tensor_tensor(own[ci][:, t, :], dh[t][:, c0:c1], 2.0, pair[:, 0, :], ALU.mult, ALU.mult)
+            if (ci, t) in ((1, 0), (1, 1), (1, 2), (1, 3)):
+                d3 = tile([P, c1 - c0], F32, f"d3_{ci}_{t}")
+                nc.scalar.activation(d3[:], dh[t][:].indirect(n3_t[:, ent]), COPY)
+                nc.vector.tensor_tensor(far[ci][:, t, :], d3[:], pair[:, 1, :], ALU.mult)
+            else:
+                nc.vector.tensor_tensor(far[ci][:, t, :], dh[t][:].indirect(n3_t[:, ent]), pair[:, 1, :], ALU.mult)
+
+        def second_product(ci, a, b, first_bank, last):
+            c0 = CHUNKS[ci][0]
+            n = b - a
+            z_b = tile([P, n, PACK], BF16, f"z_b{c0 + a}")
+            nc.vector.tensor_tensor(
+                z_b[:].rearrange("p (c i) t -> p c t i", i=4),
+                own[ci][:, :, a:b].rearrange("p t (c i) -> p c t i", i=4),
+                far[ci][:, :, a:b].rearrange("p t (c i) -> p c t i", i=4),
+                ALU.add,
+            )
+            z_w, z_s = quantize(z_b[:].rearrange("p c t -> p (c t)"), n, f"z{c0 + a}")
+            for t in range(PACK):
+                bank = psum.tile([P, S], F32, name=f"h_ps{c0 + a}_{t}", tag=f"bank{first_bank + t}")
+                product(bank[:, :n], w2_w, w2_s, t, z_w[:], z_s[:])
+                if last and t > 0:
+                    nc.vector.tensor_copy(h_rows[t][:, c0 + a : c0 + b], bank[:, :n])
+                else:
+                    nc.scalar.copy(h_rows[t][:, c0 + a : c0 + b], bank[:, :n])
+
+        steps = [(ci, t) for ci in range(len(CHUNKS)) for t in range(PACK)]
+        differences(*steps[0])
+        for i, (ci, t) in enumerate(steps):
+            if i + 1 < len(steps):
+                differences(*steps[i + 1])
+            products(ci, t)
+            if t == PACK - 1 and ci == 0:
+                second_product(0, 0, 256, 0, False)
+        second_product(1, 0, 128, 4, False)
+        second_product(1, 128, 256, 0, True)
+
+        ra = []
+
+        def fetch(t):
+            old = tile([P, W], F32, f"old{t}")
+            nc.scalar.activation(old[:], h_rows[t][:].indirect(n4_t[:]), COPY)
+            pa = tile([P, W], F32, f"pa{t}")
+            nc.vector.tensor_copy(pa[:], h_rows[t][:].indirect(n5_t[:]))
+            r = tile([P, W], F32, f"ra{t}")
+            nc.vector.scalar_tensor_tensor(r[:], old[:], 0.5, pa[:], ALU.mult, ALU.max)
+            ra.append(r)
+
+        def put(t):
+            nc.scalar.activation(h_rows[t][:].indirect(n4_t[:]), ra[t][:], COPY)
+            nc.sync.dma_start(out[P * t : P * (t + 1), :], h_rows[t][:])
+
+        fetch(0)
+        for t in range(PACK):
+            if t + 1 < PACK:
+                fetch(t + 1)
+            put(t)

@@ -17,7 +17,8 @@ PACK = 4
 T = 2048
 S = 512
 W = 384
-CHUNKS = ((0, 256), (256, 512))
+HALF = S // 2
+AHEAD = 3
 FLOPS = 3 * 2 * 512 * 512 * 512
 
 
@@ -26,15 +27,19 @@ def tile_picked_twkeyflowbkmax_none_p_kernel(tc, x_words, x_scales, w1, d_words,
     with ExitStack() as ctx:
         lists = ctx.enter_context(tc.tile_pool(name="lists", bufs=1))
         sb = ctx.enter_context(tc.tile_pool(name="sb", bufs=1))
+        reuse = ctx.enter_context(tc.tile_pool(name="reuse", bufs=1))
         psum = ctx.enter_context(tc.psum_pool(name="psum", bufs=1))
+
+        def tile(shape, dtype, name, tag="", bufs=1):
+            return sb.tile(shape, dtype, name=name, tag=tag or name, bufs=bufs, align_bytes=64)
+
+        def placed(shape, dtype, name, offset):
+            return reuse.tile(shape, dtype, name=name, align_bytes=64, offset=offset)
 
         def load_list(src, name):
             t = lists.tile(list(src.shape), U16, name=name)
             nc.sync.dma_start(t[:], src)
             return t
-
-        def tile(shape, dtype, name, tag="", bufs=1):
-            return sb.tile(shape, dtype, name=name, tag=tag or name, bufs=bufs, align_bytes=64)
 
         def load_weight(src, name):
             t = tile([P, PACK, S], F32, name)
@@ -48,17 +53,17 @@ def tile_picked_twkeyflowbkmax_none_p_kernel(tc, x_words, x_scales, w1, d_words,
 
         xs_tab = tile([P, T], U8, "xs_tab")
         ds_tab = tile([P, T], U8, "ds_tab")
-        nc.vector.memset(ds_tab[:].bitcast(I32), 0)
-        nc.gpsimd.memset(xs_tab[:].bitcast(I32), 0)
-        k1_t = load_list(k1, "k1_t")
-        offs_t = load_list(offs, "offs_t")
+        nc.vector.memset(xs_tab[:].bitcast(I32), 0)
+        nc.gpsimd.memset(ds_tab[:].bitcast(I32), 0)
         two_t = load_list(two, "two_t")
+        offs_t = load_list(offs, "offs_t")
+        k1_t = load_list(k1, "k1_t")
         w1_raw = load_weight(w1, "w1_raw")
-        for e in range(2):
-            nc.scalar.dma_start(ds_tab[e:P:16, :].bitcast(I32), d_scales[0, e:16:2, :].bitcast(I32))
         for q in range(4):
             nc.scalar.dma_start(xs_tab[32 * q : 32 * q + 4, :].bitcast(I32), x_scales[0, 4 * q : 4 * q + 4, :].bitcast(I32))
         xw_tab = load_words(x_words, "xw_tab")
+        for e in range(2):
+            nc.sync.dma_start(ds_tab[e:P:16, :].bitcast(I32), d_scales[0, e:16:2, :].bitcast(I32))
         n1_t = load_list(n1, "n1_t")
         n2_t = load_list(n2, "n2_t")
         dw_tab = load_words(d_words, "dw_tab")
@@ -69,36 +74,34 @@ def tile_picked_twkeyflowbkmax_none_p_kernel(tc, x_words, x_scales, w1, d_words,
         gain = tile([P, PACK], F32, "gain")
         nc.gpsimd.dma_start(gain[:], gn.rearrange("(p j) o -> p (j o)", j=PACK))
 
-        def gather_words(tab, lst, name, tag=""):
-            g = tile([P, S], I32, name, tag)
+        def gather_words(tab, lst, g):
             nc.vector.tensor_copy(g[:].bitcast(U32), tab[:].bitcast(U32).indirect(lst[:]))
             return g
 
-        def gather_bytes(tab, lst, name):
-            g = tile([P, S], U8, name)
+        def gather_bytes(tab, lst, g):
             nc.vector.tensor_copy(g[:], tab[:].indirect(lst[:]))
             return g
 
-        def quantize(src, n, name):
-            words = tile([P, n], I32, name + "_w")
-            scales = tile([P, n], U8, name + "_s")
+        def quantize(src, words, name):
+            scales = tile(list(words.shape), U8, name)
             nc.vector.quantize_mx(words[:].bitcast(FP8X4), scales[:], src)
-            return words, scales
+            return scales
 
         def product(bank, lw, ls, t, rw, rs):
             cols = slice(P * t, P * (t + 1))
-            nc.tensor.matmul_mx(bank, lhsT=lw[:, cols].bitcast(FP8X4), lhsT_scale=ls[:, cols], rhs=rw.bitcast(FP8X4), rhs_scale=rs, start=True, stop=True)
+            nc.tensor.matmul_mx(bank, lhsT=lw[:, cols].bitcast(FP8X4), lhsT_scale=ls[:, cols], rhs=rw[:].bitcast(FP8X4), rhs_scale=rs[:], start=True, stop=True)
 
-        w1_b = tile([P, PACK, P, PACK], BF16, "w1_b")
+        w1_b = placed([P, PACK, P, PACK], BF16, "w1_b", 0)
         nc.scalar.copy(w1_b[:].rearrange("p t m j -> p m j t"), w1_raw[:].rearrange("p j (m t) -> p m j t", t=PACK))
-        xq_w = gather_words(xw_tab, offs_t, "xq_w")
-        w1_w, w1_s = quantize(w1_b[:].rearrange("p t m j -> p (t m j)"), S, "w1")
+        xq_w = gather_words(xw_tab, offs_t, tile([P, S], I32, "xq_w"))
+        w1_w = tile([P, S], I32, "w1_w")
+        w1_s = quantize(w1_b[:].rearrange("p t m j -> p (t m j)"), w1_w, "w1_s")
+        xq_s = gather_bytes(xs_tab, offs_t, tile([P, S], U8, "xq_s"))
+        x2_s = gather_bytes(xs_tab, two_t, tile([P, S], U8, "x2_s"))
 
-        ds_g = gather_bytes(ds_tab, k1_t, "ds_g")
-        xq_s = gather_bytes(xs_tab, offs_t, "xq_s")
-        ds_deal = tile([P, S], U8, "ds_deal")
+        ds_g = gather_bytes(ds_tab, k1_t, placed([P, S], U8, "ds_g", 512))
+        ds_deal = placed([P, S], U8, "ds_deal", 0)
         nc.vector.tensor_copy(ds_deal[:].rearrange("p (t m) -> p m t", t=PACK), ds_g[:].rearrange("p (m t) -> p m t", t=PACK))
-        x2_s = gather_bytes(xs_tab, two_t, "x2_s")
         dk_s = tile([P, S], U8, "dk_s")
         nc.vector.tensor_copy(dk_s[:].bitcast(I32), ds_deal[:].bitcast(I32))
         for e in range(2):
@@ -107,12 +110,12 @@ def tile_picked_twkeyflowbkmax_none_p_kernel(tc, x_words, x_scales, w1, d_words,
         y_ps = []
         for t in range(PACK):
             bank = psum.tile([P, S], F32, name=f"y_ps{t}", tag=f"bank{t}")
-            product(bank[:], w1_w, w1_s, t, xq_w[:], xq_s[:])
+            product(bank[:], w1_w, w1_s, t, xq_w, xq_s)
             y_ps.append(bank)
 
-        x2_w = gather_words(xw_tab, two_t, "x2_w")
-        dw_g = gather_words(dw_tab, k1_t, "dw_g")
-        dk_w = tile([P, S], I32, "dk_w", "work")
+        x2_w = gather_words(xw_tab, two_t, placed([P, S], I32, "x2_w", 1024))
+        dw_g = gather_words(dw_tab, k1_t, placed([P, S], I32, "dw_g", 3072))
+        dk_w = tile([P, S], I32, "dk_w", f"rows{PACK - 1}")
         nc.vector.tensor_copy(dk_w[:].rearrange("p (t m) -> p m t", t=PACK), dw_g[:].rearrange("p (m t) -> p m t", t=PACK))
 
         gain32 = tile([P, PACK], F32, "gain32")
@@ -121,78 +124,91 @@ def tile_picked_twkeyflowbkmax_none_p_kernel(tc, x_words, x_scales, w1, d_words,
         dh = []
         for t in range(PACK):
             bank = psum.tile([P, S], F32, name=f"d_ps{t}", tag=f"bank{PACK + t}")
-            product(bank[:], dk_w, dk_s, t, x2_w[:], x2_s[:])
+            product(bank[:], dk_w, dk_s, t, x2_w, x2_s)
             d_t = tile([P, S], F32, f"dh{t}")
-            if t < 4:
+            if t < 0:
                 nc.vector.tensor_scalar(d_t[:], bank[:], gain32[:, t : t + 1], None, ALU.mult)
             else:
                 nc.scalar.activation(d_t[:], bank[:], COPY, scale=gain32[:, t : t + 1])
             dh.append(d_t)
 
         w2_b = tile([P, S, PACK], BF16, "w2_b")
-        nc.scalar.copy(w2_b[:].rearrange("p (c i) j -> p c j i", i=4), w2_raw[:].rearrange("p j (c i) -> p c j i", i=4))
-        w2_w, w2_s = quantize(w2_b[:].rearrange("p c j -> p (c j)"), S, "w2")
+        for t in range(PACK):
+            cols = slice(P * t, P * (t + 1))
+            nc.gpsimd.tensor_scalar(
+                w2_b[:, cols].rearrange("p (g i) j -> p g j i", i=4), w2_raw[:, :, cols].rearrange("p j (g i) -> p g j i", i=4), 1.0, 0.0, ALU.mult, ALU.add
+            )
 
-        y = [tile([P, S], F32, f"y{t}") for t in range(PACK)]
-        h_rows = [tile([P, S], F32, f"h{t}") for t in range(PACK)]
-        own = [tile([P, PACK, c1 - c0], F32, f"own{c0}") for c0, c1 in CHUNKS]
-        far = [tile([P, PACK, c1 - c0], F32, f"far{c0}") for c0, c1 in CHUNKS]
-        diff = tile([P, len(CHUNKS) * PACK, 2, 256], F32, "diff", "work")
-        pairs = {}
+        y = [tile([P, S], F32, f"y{t}", f"rows{t}") for t in range(PACK)]
+        own = [tile([P, PACK, HALF], F32, f"own{c}") for c in range(2)]
+        far = [tile([P, PACK, HALF], F32, f"far{c}") for c in range(2)]
+        first_diffs = placed([P, AHEAD, 2, HALF], F32, "first_diffs", 3072)
+        later_diffs = tile([P, 2 * PACK - AHEAD, 2, HALF], F32, "later_diffs")
+        steps = [(c, t) for c in range(2) for t in range(PACK)]
+        diffs = [first_diffs[:, i] if i < AHEAD else later_diffs[:, i - AHEAD] for i in range(len(steps))]
 
-        def differences(ci, t):
-            c0, c1 = CHUNKS[ci]
-            n = c1 - c0
-            ent = slice(c0 // 16, c1 // 16)
-            if ci == 0:
+        def differences(i):
+            c, t = steps[i]
+            ent = slice(c * HALF // 16, (c + 1) * HALF // 16)
+            if c == 0:
                 nc.scalar.copy(y[t][:], y_ps[t][:])
-            pair = tile([P, 2, n], F32, f"pair{ci}_{t}", "pair", 3)
+            pair = tile([P, 2, HALF], F32, f"pair{i}", "pair", AHEAD)
             nc.scalar.activation(pair[:, 0, :], y[t][:].indirect(n1_t[:, ent]), COPY)
             nc.scalar.activation(pair[:, 1, :], y[t][:].indirect(n2_t[:, ent]), COPY)
-            pairs[ci, t] = diff[:, PACK * ci + t]
-            nc.vector.tensor_tensor(pairs[ci, t], pair[:], y[t][:, c0:c1].unsqueeze(1).to_broadcast([P, 2, n]), ALU.subtract)
+            here = y_ps[t][:, c * HALF : (c + 1) * HALF].unsqueeze(1).to_broadcast([P, 2, HALF])
+            nc.vector.tensor_tensor(diffs[i], pair[:], here, ALU.subtract)
 
-        def products(ci, t):
-            c0, c1 = CHUNKS[ci]
-            ent = slice(c0 // 16, c1 // 16)
-            pair = pairs[ci, t]
-            nc.vector.scalar_tensor_tensor(own[ci][:, t, :], dh[t][:, c0:c1], 2.0, pair[:, 0, :], ALU.mult, ALU.mult)
-            if (ci, t) in ((1, 0), (1, 1), (1, 2), (1, 3)):
-                d3 = tile([P, c1 - c0], F32, f"d3_{ci}_{t}")
+        def products(i):
+            c, t = steps[i]
+            ent = slice(c * HALF // 16, (c + 1) * HALF // 16)
+            nc.vector.scalar_tensor_tensor(own[c][:, t, :], dh[t][:, c * HALF : (c + 1) * HALF], 2.0, diffs[i][:, 0, :], ALU.mult, ALU.mult)
+            if i in (6, 7):
+                d3 = tile([P, HALF], F32, f"d3_{i}", "pair", AHEAD)
                 nc.scalar.activation(d3[:], dh[t][:].indirect(n3_t[:, ent]), COPY)
-                nc.vector.tensor_tensor(far[ci][:, t, :], d3[:], pair[:, 1, :], ALU.mult)
+                nc.vector.tensor_tensor(far[c][:, t, :], d3[:], diffs[i][:, 1, :], ALU.mult)
             else:
-                nc.vector.tensor_tensor(far[ci][:, t, :], dh[t][:].indirect(n3_t[:, ent]), pair[:, 1, :], ALU.mult)
+                nc.vector.tensor_tensor(far[c][:, t, :], dh[t][:].indirect(n3_t[:, ent]), diffs[i][:, 1, :], ALU.mult)
 
-        def second_product(ci, a, b, first_bank, last):
-            c0 = CHUNKS[ci][0]
+        def second_product(c, a, b, first_bank):
             n = b - a
-            z_b = tile([P, n, PACK], BF16, f"z_b{c0 + a}")
+            j0 = c * HALF + a
+            z_b = tile([P, n, PACK], BF16, f"z_b{j0}")
             nc.vector.tensor_tensor(
-                z_b[:].rearrange("p (c i) t -> p c t i", i=4),
-                own[ci][:, :, a:b].rearrange("p t (c i) -> p c t i", i=4),
-                far[ci][:, :, a:b].rearrange("p t (c i) -> p c t i", i=4),
+                z_b[:].rearrange("p (g i) t -> p g t i", i=4),
+                own[c][:, :, a:b].rearrange("p t (g i) -> p g t i", i=4),
+                far[c][:, :, a:b].rearrange("p t (g i) -> p g t i", i=4),
                 ALU.add,
             )
-            z_w, z_s = quantize(z_b[:].rearrange("p c t -> p (c t)"), n, f"z{c0 + a}")
+            z_w = tile([P, n], I32, f"z_w{j0}")
+            z_s = quantize(z_b[:].rearrange("p g t -> p (g t)"), z_w, f"z_s{j0}")
+            banks = []
             for t in range(PACK):
-                bank = psum.tile([P, S], F32, name=f"h_ps{c0 + a}_{t}", tag=f"bank{first_bank + t}")
-                product(bank[:, :n], w2_w, w2_s, t, z_w[:], z_s[:])
-                if last and t > 0:
-                    nc.vector.tensor_copy(h_rows[t][:, c0 + a : c0 + b], bank[:, :n])
-                else:
-                    nc.scalar.copy(h_rows[t][:, c0 + a : c0 + b], bank[:, :n])
+                bank = psum.tile([P, S], F32, name=f"h_ps{j0}_{t}", tag=f"bank{first_bank + t}")
+                product(bank[:, :n], w2_w, w2_s, t, z_w, z_s)
+                banks.append(bank)
+            return banks
 
-        steps = [(ci, t) for ci in range(len(CHUNKS)) for t in range(PACK)]
-        differences(*steps[0])
-        for i, (ci, t) in enumerate(steps):
+        differences(0)
+        for i in range(len(steps)):
             if i + 1 < len(steps):
-                differences(*steps[i + 1])
-            products(ci, t)
-            if t == PACK - 1 and ci == 0:
-                second_product(0, 0, 256, 0, False)
-        second_product(1, 0, 128, 4, False)
-        second_product(1, 128, 256, 0, True)
+                differences(i + 1)
+            products(i)
+            if i == AHEAD - 1:
+                w2_w = placed([P, S], I32, "w2_w", 3072)
+                w2_s = quantize(w2_b[:].rearrange("p g j -> p (g j)"), w2_w, "w2_s")
+            if i == PACK - 1:
+                h_first = second_product(0, 0, HALF, PACK)
+
+        h_rows = [tile([P, S], F32, f"h{t}", f"rows{t}") for t in range(PACK)]
+        for t in range(PACK):
+            nc.scalar.copy(h_rows[t][:, :HALF], h_first[t][:, :HALF])
+        h_third = second_product(1, 0, P, 0)
+        for t in range(PACK):
+            nc.scalar.copy(h_rows[t][:, HALF : HALF + P], h_third[t][:, :P])
+        h_last = second_product(1, P, HALF, PACK)
+        nc.scalar.copy(h_rows[0][:, HALF + P :], h_last[0][:, :P])
+        for t in range(1, PACK):
+            nc.vector.tensor_copy(h_rows[t][:, HALF + P :], h_last[t][:, :P])
 
         ra = []
 

@@ -91,17 +91,18 @@ def tile_picked_twkeyflowbkmax_none_p_kernel(tc, x_words, x_scales, w1, d_words,
             cols = slice(P * t, P * (t + 1))
             nc.tensor.matmul_mx(bank, lhsT=lw[:, cols].bitcast(FP8X4), lhsT_scale=ls[:, cols], rhs=rw[:].bitcast(FP8X4), rhs_scale=rs[:], start=True, stop=True)
 
-        w1_b = placed([P, PACK, P, PACK], BF16, "w1_b", 0)
-        nc.scalar.copy(w1_b[:].rearrange("p t m j -> p m j t"), w1_raw[:].rearrange("p j (m t) -> p m j t", t=PACK))
+        w1_b = placed([P, PACK, P, PACK], BF16, "w1_b", 8192)
+        for u in range(0, PACK, 2):
+            nc.scalar.copy(w1_b[:, u : u + 2].rearrange("p t m j -> p m j t"), w1_raw[:].rearrange("p j (m t) -> p m j t", t=PACK)[:, :, :, u : u + 2])
         xq_w = gather_words(xw_tab, offs_t, tile([P, S], I32, "xq_w"))
         w1_w = tile([P, S], I32, "w1_w")
         w1_s = quantize(w1_b[:].rearrange("p t m j -> p (t m j)"), w1_w, "w1_s")
         xq_s = gather_bytes(xs_tab, offs_t, tile([P, S], U8, "xq_s"))
         x2_s = gather_bytes(xs_tab, two_t, tile([P, S], U8, "x2_s"))
 
-        ds_g = gather_bytes(ds_tab, k1_t, placed([P, S], U8, "ds_g", 512))
-        ds_deal = placed([P, S], U8, "ds_deal", 0)
-        nc.vector.tensor_copy(ds_deal[:].rearrange("p (t m) -> p m t", t=PACK), ds_g[:].rearrange("p (m t) -> p m t", t=PACK))
+        ds_g = gather_bytes(ds_tab, k1_t, placed([P, S], U8, "ds_g", 9728))
+        ds_deal = placed([P, S], U8, "ds_deal", 9216)
+        nc.vector.tensor_copy(ds_deal[:].rearrange("p (t m) -> p t m", t=PACK), ds_g[:].rearrange("p (m t) -> p t m", t=PACK))
         dk_s = tile([P, S], U8, "dk_s")
         nc.vector.tensor_copy(dk_s[:].bitcast(I32), ds_deal[:].bitcast(I32))
         for e in range(2):
@@ -113,10 +114,10 @@ def tile_picked_twkeyflowbkmax_none_p_kernel(tc, x_words, x_scales, w1, d_words,
             product(bank[:], w1_w, w1_s, t, xq_w, xq_s)
             y_ps.append(bank)
 
-        x2_w = gather_words(xw_tab, two_t, placed([P, S], I32, "x2_w", 1024))
-        dw_g = gather_words(dw_tab, k1_t, placed([P, S], I32, "dw_g", 3072))
+        x2_w = gather_words(xw_tab, two_t, placed([P, S], I32, "x2_w", 10240))
+        dw_g = gather_words(dw_tab, k1_t, placed([P, S], I32, "dw_g", 7168))
         dk_w = tile([P, S], I32, "dk_w", f"rows{PACK - 1}")
-        nc.vector.tensor_copy(dk_w[:].rearrange("p (t m) -> p m t", t=PACK), dw_g[:].rearrange("p (m t) -> p m t", t=PACK))
+        nc.vector.tensor_copy(dk_w[:].rearrange("p (t g i) -> p g t i", t=PACK, i=4), dw_g[:].rearrange("p (g i t) -> p g t i", t=PACK, i=4))
 
         gain32 = tile([P, PACK], F32, "gain32")
         nc.gpsimd.tensor_scalar(gain32[:], gain[:], 0.03125, 0.0, ALU.mult, ALU.add)
@@ -136,14 +137,16 @@ def tile_picked_twkeyflowbkmax_none_p_kernel(tc, x_words, x_scales, w1, d_words,
         for t in range(PACK):
             cols = slice(P * t, P * (t + 1))
             nc.gpsimd.tensor_scalar(
-                w2_b[:, cols].rearrange("p (g i) j -> p g j i", i=4), w2_raw[:, :, cols].rearrange("p j (g i) -> p g j i", i=4), 1.0, 0.0, ALU.mult, ALU.add
+                w2_b[:, cols].rearrange("p (g i) j -> p g j i", i=2), w2_raw[:, :, cols].rearrange("p j (g i) -> p g j i", i=2), 1.0, 0.0, ALU.mult, ALU.add
             )
 
         y = [tile([P, S], F32, f"y{t}", f"rows{t}") for t in range(PACK)]
         own = [tile([P, PACK, HALF], F32, f"own{c}") for c in range(2)]
         far = [tile([P, PACK, HALF], F32, f"far{c}") for c in range(2)]
-        first_diffs = placed([P, AHEAD, 2, HALF], F32, "first_diffs", 3072)
+        first_diffs = placed([P, AHEAD, 2, HALF], F32, "first_diffs", 2048)
         later_diffs = tile([P, 2 * PACK - AHEAD, 2, HALF], F32, "later_diffs")
+        first_pairs = tile([P, AHEAD, 2, HALF], F32, "first_pairs")
+        later_pairs = placed([P, 2 * PACK - AHEAD, 2, HALF], F32, "later_pairs", 10240)
         steps = [(c, t) for c in range(2) for t in range(PACK)]
         diffs = [first_diffs[:, i] if i < AHEAD else later_diffs[:, i - AHEAD] for i in range(len(steps))]
 
@@ -152,18 +155,18 @@ def tile_picked_twkeyflowbkmax_none_p_kernel(tc, x_words, x_scales, w1, d_words,
             ent = slice(c * HALF // 16, (c + 1) * HALF // 16)
             if c == 0:
                 nc.scalar.copy(y[t][:], y_ps[t][:])
-            pair = tile([P, 2, HALF], F32, f"pair{i}", "pair", AHEAD)
+            pair = first_pairs[:, i] if i < AHEAD else later_pairs[:, i - AHEAD]
             nc.scalar.activation(pair[:, 0, :], y[t][:].indirect(n1_t[:, ent]), COPY)
             nc.scalar.activation(pair[:, 1, :], y[t][:].indirect(n2_t[:, ent]), COPY)
             here = y_ps[t][:, c * HALF : (c + 1) * HALF].unsqueeze(1).to_broadcast([P, 2, HALF])
-            nc.vector.tensor_tensor(diffs[i], pair[:], here, ALU.subtract)
+            nc.vector.tensor_tensor(diffs[i], pair, here, ALU.subtract)
 
         def products(i):
             c, t = steps[i]
             ent = slice(c * HALF // 16, (c + 1) * HALF // 16)
             nc.vector.scalar_tensor_tensor(own[c][:, t, :], dh[t][:, c * HALF : (c + 1) * HALF], 2.0, diffs[i][:, 0, :], ALU.mult, ALU.mult)
-            if i in (6, 7):
-                d3 = tile([P, HALF], F32, f"d3_{i}", "pair", AHEAD)
+            if i in (4, 5, 6, 7):
+                d3 = tile([P, HALF], F32, f"d3_{i}", "")
                 nc.scalar.activation(d3[:], dh[t][:].indirect(n3_t[:, ent]), COPY)
                 nc.vector.tensor_tensor(far[c][:, t, :], d3[:], diffs[i][:, 1, :], ALU.mult)
             else:
@@ -174,9 +177,9 @@ def tile_picked_twkeyflowbkmax_none_p_kernel(tc, x_words, x_scales, w1, d_words,
             j0 = c * HALF + a
             z_b = tile([P, n, PACK], BF16, f"z_b{j0}")
             nc.vector.tensor_tensor(
-                z_b[:].rearrange("p (g i) t -> p g t i", i=4),
-                own[c][:, :, a:b].rearrange("p t (g i) -> p g t i", i=4),
-                far[c][:, :, a:b].rearrange("p t (g i) -> p g t i", i=4),
+                z_b[:].rearrange("p (g i) t -> p g t i", i=2),
+                own[c][:, :, a:b].rearrange("p t (g i) -> p g t i", i=2),
+                far[c][:, :, a:b].rearrange("p t (g i) -> p g t i", i=2),
                 ALU.add,
             )
             z_w = tile([P, n], I32, f"z_w{j0}")
@@ -190,11 +193,13 @@ def tile_picked_twkeyflowbkmax_none_p_kernel(tc, x_words, x_scales, w1, d_words,
 
         differences(0)
         for i in range(len(steps)):
-            if i + 1 < len(steps):
+            if i + 1 < len(steps) and i != PACK - 1:
                 differences(i + 1)
             products(i)
+            if i == PACK - 1:
+                differences(i + 1)
             if i == AHEAD - 1:
-                w2_w = placed([P, S], I32, "w2_w", 3072)
+                w2_w = placed([P, S], I32, "w2_w", 2048)
                 w2_s = quantize(w2_b[:].rearrange("p g j -> p (g j)"), w2_w, "w2_s")
             if i == PACK - 1:
                 h_first = second_product(0, 0, HALF, PACK)
@@ -207,12 +212,12 @@ def tile_picked_twkeyflowbkmax_none_p_kernel(tc, x_words, x_scales, w1, d_words,
             nc.scalar.copy(h_rows[t][:, HALF : HALF + P], h_third[t][:, :P])
         h_last = second_product(1, P, HALF, PACK)
         nc.scalar.copy(h_rows[0][:, HALF + P :], h_last[0][:, :P])
-        for t in range(1, PACK):
-            nc.vector.tensor_copy(h_rows[t][:, HALF + P :], h_last[t][:, :P])
 
         ra = []
 
         def fetch(t):
+            if t + 1 < PACK:
+                nc.vector.tensor_copy(h_rows[t + 1][:, HALF + P :], h_last[t + 1][:, :P])
             old = tile([P, W], F32, f"old{t}")
             nc.scalar.activation(old[:], h_rows[t][:].indirect(n4_t[:]), COPY)
             pa = tile([P, W], F32, f"pa{t}")

from contextlib import ExitStack

import concourse.mybir as mybir

F32 = mybir.dt.float32
BF16 = mybir.dt.bfloat16
I32 = mybir.dt.int32
U32 = mybir.dt.uint32
U16 = mybir.dt.uint16
U8 = mybir.dt.uint8
FP8X4 = mybir.dt.float8_e4m3fn_x4
ALU = mybir.AluOpType
COPY = mybir.ActivationFunctionType.Copy

P = 128
PACK = 4
T = 2048
S = 512
W = 384
HALF = S // 2
AHEAD = 3
FLOPS = 3 * 2 * 512 * 512 * 512


def tile_picked_twkeyflowbkmax_none_p_kernel(tc, x_words, x_scales, w1, d_words, d_scales, gn, w2, offs, k1, two, n1, n2, n3, n4, n5, out):
    nc = tc.nc
    with ExitStack() as ctx:
        lists = ctx.enter_context(tc.tile_pool(name="lists", bufs=1))
        sb = ctx.enter_context(tc.tile_pool(name="sb", bufs=1))
        reuse = ctx.enter_context(tc.tile_pool(name="reuse", bufs=1))
        psum = ctx.enter_context(tc.psum_pool(name="psum", bufs=1))

        def tile(shape, dtype, name, tag="", bufs=1):
            return sb.tile(shape, dtype, name=name, tag=tag or name, bufs=bufs, align_bytes=64)

        def placed(shape, dtype, name, offset):
            return reuse.tile(shape, dtype, name=name, align_bytes=64, offset=offset)

        def load_list(src, name):
            t = lists.tile(list(src.shape), U16, name=name)
            nc.sync.dma_start(t[:], src)
            return t

        def load_weight(src, name):
            t = tile([P, PACK, S], F32, name)
            nc.sync.dma_start(t[:], src.rearrange("(p j) c -> p j c", j=PACK))
            return t

        def load_words(src, name):
            t = tile([P, T], I32, name)
            nc.sync.dma_start(t[:], src[0].rearrange("p n t -> p (n t)").bitcast(I32))
            return t

        xs_tab = tile([P, T], U8, "xs_tab")
        ds_tab = tile([P, T], U8, "ds_tab")
        nc.vector.memset(xs_tab[:].bitcast(I32), 0)
        nc.gpsimd.memset(ds_tab[:].bitcast(I32), 0)
        two_t = load_list(two, "two_t")
        offs_t = load_list(offs, "offs_t")
        k1_t = load_list(k1, "k1_t")
        w1_raw = load_weight(w1, "w1_raw")
        for q in range(4):
            nc.scalar.dma_start(xs_tab[32 * q : 32 * q + 4, :].bitcast(I32), x_scales[0, 4 * q : 4 * q + 4, :].bitcast(I32))
        xw_tab = load_words(x_words, "xw_tab")
        for e in range(2):
            nc.sync.dma_start(ds_tab[e:P:16, :].bitcast(I32), d_scales[0, e:16:2, :].bitcast(I32))
        n1_t = load_list(n1, "n1_t")
        n2_t = load_list(n2, "n2_t")
        dw_tab = load_words(d_words, "dw_tab")
        w2_raw = load_weight(w2, "w2_raw")
        n3_t = load_list(n3, "n3_t")
        n4_t = load_list(n4, "n4_t")
        n5_t = load_list(n5, "n5_t")
        gain = tile([P, PACK], F32, "gain")
        nc.gpsimd.dma_start(gain[:], gn.rearrange("(p j) o -> p (j o)", j=PACK))

        def gather_words(tab, lst, g):
            nc.vector.tensor_copy(g[:].bitcast(U32), tab[:].bitcast(U32).indirect(lst[:]))
            return g

        def gather_bytes(tab, lst, g):
            nc.vector.tensor_copy(g[:], tab[:].indirect(lst[:]))
            return g

        def quantize(src, words, name):
            scales = tile(list(words.shape), U8, name)
            nc.vector.quantize_mx(words[:].bitcast(FP8X4), scales[:], src)
            return scales

        def product(bank, lw, ls, t, rw, rs):
            cols = slice(P * t, P * (t + 1))
            nc.tensor.matmul_mx(bank, lhsT=lw[:, cols].bitcast(FP8X4), lhsT_scale=ls[:, cols], rhs=rw[:].bitcast(FP8X4), rhs_scale=rs[:], start=True, stop=True)

        w1_b = placed([P, PACK, P, PACK], BF16, "w1_b", 8192)
        for u in range(0, PACK, 2):
            nc.scalar.copy(w1_b[:, u : u + 2].rearrange("p t m j -> p m j t"), w1_raw[:].rearrange("p j (m t) -> p m j t", t=PACK)[:, :, :, u : u + 2])
        xq_w = gather_words(xw_tab, offs_t, tile([P, S], I32, "xq_w"))
        w1_w = tile([P, S], I32, "w1_w")
        w1_s = quantize(w1_b[:].rearrange("p t m j -> p (t m j)"), w1_w, "w1_s")
        xq_s = gather_bytes(xs_tab, offs_t, tile([P, S], U8, "xq_s"))
        x2_s = gather_bytes(xs_tab, two_t, tile([P, S], U8, "x2_s"))

        ds_g = gather_bytes(ds_tab, k1_t, placed([P, S], U8, "ds_g", 9728))
        ds_deal = placed([P, S], U8, "ds_deal", 9216)
        nc.vector.tensor_copy(ds_deal[:].rearrange("p (t m) -> p t m", t=PACK), ds_g[:].rearrange("p (m t) -> p t m", t=PACK))
        dk_s = tile([P, S], U8, "dk_s")
        nc.vector.tensor_copy(dk_s[:].bitcast(I32), ds_deal[:].bitcast(I32))
        for e in range(2):
            nc.sync.dma_start(dk_s[2 + e : P : 32, :].bitcast(I32), ds_deal[16 + e : P : 32, :].bitcast(I32))

        y_ps = []
        for t in range(PACK):
            bank = psum.tile([P, S], F32, name=f"y_ps{t}", tag=f"bank{t}")
            product(bank[:], w1_w, w1_s, t, xq_w, xq_s)
            y_ps.append(bank)

        x2_w = gather_words(xw_tab, two_t, placed([P, S], I32, "x2_w", 10240))
        dw_g = gather_words(dw_tab, k1_t, placed([P, S], I32, "dw_g", 7168))
        dk_w = tile([P, S], I32, "dk_w", f"rows{PACK - 1}")
        nc.vector.tensor_copy(dk_w[:].rearrange("p (t g i) -> p g t i", t=PACK, i=4), dw_g[:].rearrange("p (g i t) -> p g t i", t=PACK, i=4))

        gain32 = tile([P, PACK], F32, "gain32")
        nc.gpsimd.tensor_scalar(gain32[:], gain[:], 0.03125, 0.0, ALU.mult, ALU.add)

        dh = []
        for t in range(PACK):
            bank = psum.tile([P, S], F32, name=f"d_ps{t}", tag=f"bank{PACK + t}")
            product(bank[:], dk_w, dk_s, t, x2_w, x2_s)
            d_t = tile([P, S], F32, f"dh{t}")
            if t < 0:
                nc.vector.tensor_scalar(d_t[:], bank[:], gain32[:, t : t + 1], None, ALU.mult)
            else:
                nc.scalar.activation(d_t[:], bank[:], COPY, scale=gain32[:, t : t + 1])
            dh.append(d_t)

        w2_b = tile([P, S, PACK], BF16, "w2_b")
        for t in range(PACK):
            cols = slice(P * t, P * (t + 1))
            nc.gpsimd.tensor_scalar(
                w2_b[:, cols].rearrange("p (g i) j -> p g j i", i=2), w2_raw[:, :, cols].rearrange("p j (g i) -> p g j i", i=2), 1.0, 0.0, ALU.mult, ALU.add
            )

        y = [tile([P, S], F32, f"y{t}", f"rows{t}") for t in range(PACK)]
        own = [tile([P, PACK, HALF], F32, f"own{c}") for c in range(2)]
        far = [tile([P, PACK, HALF], F32, f"far{c}") for c in range(2)]
        first_diffs = placed([P, AHEAD, 2, HALF], F32, "first_diffs", 2048)
        later_diffs = tile([P, 2 * PACK - AHEAD, 2, HALF], F32, "later_diffs")
        first_pairs = tile([P, AHEAD, 2, HALF], F32, "first_pairs")
        later_pairs = placed([P, 2 * PACK - AHEAD, 2, HALF], F32, "later_pairs", 10240)
        steps = [(c, t) for c in range(2) for t in range(PACK)]
        diffs = [first_diffs[:, i] if i < AHEAD else later_diffs[:, i - AHEAD] for i in range(len(steps))]

        def differences(i):
            c, t = steps[i]
            ent = slice(c * HALF // 16, (c + 1) * HALF // 16)
            if c == 0:
                nc.scalar.copy(y[t][:], y_ps[t][:])
            pair = first_pairs[:, i] if i < AHEAD else later_pairs[:, i - AHEAD]
            nc.scalar.activation(pair[:, 0, :], y[t][:].indirect(n1_t[:, ent]), COPY)
            nc.scalar.activation(pair[:, 1, :], y[t][:].indirect(n2_t[:, ent]), COPY)
            here = y_ps[t][:, c * HALF : (c + 1) * HALF].unsqueeze(1).to_broadcast([P, 2, HALF])
            nc.vector.tensor_tensor(diffs[i], pair, here, ALU.subtract)

        def products(i):
            c, t = steps[i]
            ent = slice(c * HALF // 16, (c + 1) * HALF // 16)
            nc.vector.scalar_tensor_tensor(own[c][:, t, :], dh[t][:, c * HALF : (c + 1) * HALF], 2.0, diffs[i][:, 0, :], ALU.mult, ALU.mult)
            if i in (4, 5, 6, 7):
                d3 = tile([P, HALF], F32, f"d3_{i}", "")
                nc.scalar.activation(d3[:], dh[t][:].indirect(n3_t[:, ent]), COPY)
                nc.vector.tensor_tensor(far[c][:, t, :], d3[:], diffs[i][:, 1, :], ALU.mult)
            else:
                nc.vector.tensor_tensor(far[c][:, t, :], dh[t][:].indirect(n3_t[:, ent]), diffs[i][:, 1, :], ALU.mult)

        def second_product(c, a, b, first_bank):
            n = b - a
            j0 = c * HALF + a
            z_b = tile([P, n, PACK], BF16, f"z_b{j0}")
            nc.vector.tensor_tensor(
                z_b[:].rearrange("p (g i) t -> p g t i", i=2),
                own[c][:, :, a:b].rearrange("p t (g i) -> p g t i", i=2),
                far[c][:, :, a:b].rearrange("p t (g i) -> p g t i", i=2),
                ALU.add,
            )
            z_w = tile([P, n], I32, f"z_w{j0}")
            z_s = quantize(z_b[:].rearrange("p g t -> p (g t)"), z_w, f"z_s{j0}")
            banks = []
            for t in range(PACK):
                bank = psum.tile([P, S], F32, name=f"h_ps{j0}_{t}", tag=f"bank{first_bank + t}")
                product(bank[:, :n], w2_w, w2_s, t, z_w, z_s)
                banks.append(bank)
            return banks

        differences(0)
        for i in range(len(steps)):
            if i + 1 < len(steps) and i != PACK - 1:
                differences(i + 1)
            products(i)
            if i == PACK - 1:
                differences(i + 1)
            if i == AHEAD - 1:
                w2_w = placed([P, S], I32, "w2_w", 2048)
                w2_s = quantize(w2_b[:].rearrange("p g j -> p (g j)"), w2_w, "w2_s")
            if i == PACK - 1:
                h_first = second_product(0, 0, HALF, PACK)

        h_rows = [tile([P, S], F32, f"h{t}", f"rows{t}") for t in range(PACK)]
        for t in range(PACK):
            nc.scalar.copy(h_rows[t][:, :HALF], h_first[t][:, :HALF])
        h_third = second_product(1, 0, P, 0)
        for t in range(PACK):
            nc.scalar.copy(h_rows[t][:, HALF : HALF + P], h_third[t][:, :P])
        h_last = second_product(1, P, HALF, PACK)
        nc.scalar.copy(h_rows[0][:, HALF + P :], h_last[0][:, :P])

        ra = []

        def fetch(t):
            if t + 1 < PACK:
                nc.vector.tensor_copy(h_rows[t + 1][:, HALF + P :], h_last[t + 1][:, :P])
            old = tile([P, W], F32, f"old{t}")
            nc.scalar.activation(old[:], h_rows[t][:].indirect(n4_t[:]), COPY)
            pa = tile([P, W], F32, f"pa{t}")
            nc.vector.tensor_copy(pa[:], h_rows[t][:].indirect(n5_t[:]))
            r = tile([P, W], F32, f"ra{t}")
            nc.vector.scalar_tensor_tensor(r[:], old[:], 0.5, pa[:], ALU.mult, ALU.max)
            ra.append(r)

        def put(t):
            nc.scalar.activation(h_rows[t][:].indirect(n4_t[:]), ra[t][:], COPY)
            nc.sync.dma_start(out[P * t : P * (t + 1), :], h_rows[t][:])

        fetch(0)
        for t in range(PACK):
            if t + 1 < PACK:
                fetch(t + 1)
            put(t)
